import numpy as np
import ml_dtypes


def mxq(x, axis, fmt="e4m3"):
    dtype, down = {"e4m3": (ml_dtypes.float8_e4m3fn, 7), "e5m2": (ml_dtypes.float8_e5m2, 14)}[fmt]
    v = np.moveaxis(np.asarray(x, np.float32).astype(ml_dtypes.bfloat16).astype(np.float64), axis, -1)
    blocks = v.reshape(v.shape[:-1] + (-1, 32))
    amax = np.abs(blocks).max(-1, keepdims=True)
    byte = np.maximum(np.where(amax > 0, np.frexp(amax)[1] - 1 + 127, 0) - down, 1)
    scale = np.exp2(byte - 127.0)
    codes = (blocks / scale).astype(np.float32).astype(dtype).astype(np.float64)
    return np.moveaxis((codes * scale).reshape(v.shape), -1, axis)


WIDE = False


def mx_kscale(k):
    if not WIDE:
        return np.ones(k)
    levels = np.array([10, -10, 5, -5, 0])
    if k % 512:
        return np.exp2(np.random.permutation(np.resize(levels, k // 32))).repeat(32)
    a = np.empty((k // 512, 16))
    for p in range(k // 512):
        a[p, :8] = np.random.permutation(np.resize(levels, 8))
        for g in range(8):
            far = levels[np.abs(levels - a[p, g]) >= 10]
            a[p, g + 8] = far[np.random.randint(len(far))]
    return np.exp2(a.ravel()).repeat(32)


def f64(x):
    return np.asarray(x).astype(np.float64)


def striped(idx):
    return np.tile(np.asarray(idx).reshape(-1, 16).T, (8, 1)).astype(np.uint16)


def unstriped(offs):
    return offs[:16].T.reshape(-1).astype(np.int64)


E2M1 = np.array([0.0, 0.5, 1.0, 1.5, 2.0, 3.0, 4.0, 6.0, -0.0, -0.5, -1.0, -1.5, -2.0, -3.0, -4.0, -6.0])


def pack_weight(w, fmt):
    k, n = w.shape
    w = f64(np.asarray(w, np.float32).astype(ml_dtypes.bfloat16)).reshape(k // 32, 32, n)
    amax = np.abs(w).max(1)
    if fmt == "e4m3":
        byte = np.frexp(amax)[1] - 1 + 127 - 7
    else:
        mant, ex = np.frexp(amax / 6.0)
        byte = np.where(mant > 0.5, ex, ex - 1) + 127
    byte = np.clip(np.where(amax > 0, byte, 1), 1, 254)
    scaled = (w * np.exp2(127.0 - byte)[:, None, :]).reshape(k, n).astype(np.float32)
    by_word = np.ascontiguousarray(scaled.reshape(k // 512, 128, 4, n).transpose(0, 1, 3, 2))
    if fmt == "e4m3":
        words = by_word.astype(ml_dtypes.float8_e4m3fn).view(np.uint8)
    else:
        c = by_word.astype(ml_dtypes.float4_e2m1fn).view(np.uint8) & 0xF
        words = (c[..., 0::2] | (c[..., 1::2] << 4)).reshape(k // 512, 128, 2 * n)
    return np.ascontiguousarray(words), np.ascontiguousarray(byte.astype(np.uint8).reshape(k // 512, 16, n))


def unpack_weight(words, scales, fmt):
    g, _, n = scales.shape
    words = np.ascontiguousarray(words).reshape(g, 128, n, -1)
    if fmt == "e4m3":
        vals = words.view(ml_dtypes.float8_e4m3fn).astype(np.float64)
    else:
        nib = np.empty((g, 128, n, 4), np.uint8)
        nib[..., 0::2] = words & 0xF
        nib[..., 1::2] = words >> 4
        vals = E2M1[nib]
    vals = vals * np.repeat(np.exp2(scales.astype(np.float64) - 127.0), 8, axis=1)[..., None]
    return vals.transpose(0, 1, 3, 2).reshape(g * 512, n)


def sigmoid(v):
    return 1.0 / (1.0 + np.exp(-v))


D, E, T, I, Q = 512, 512, 2048, 512, 128


def setup_inputs():
    n = np.random.standard_normal
    idx = np.random.permutation(T)[:I]
    fd = mx_kscale(D)
    fi = mx_kscale(I)
    ti = np.ones(T)
    ti[idx] = fi
    keysp = pack_weight(n((D, T)) / fd[:, None], "e4m3")
    return {
        "query": (n((D, Q)) * 0.8 / np.sqrt(D) * fd[:, None]).astype(np.float32),
        "keys_words": keysp[0],
        "keys_scales": keysp[1],
        "th": (np.random.uniform(0.4, 1.0, (Q, 1))).astype(np.float32),
        "dquery": (n((D, Q)) * 0.6 / np.sqrt(D) * fd[:, None]).astype(np.float32),
        "os": (np.random.uniform(4.0, 16.0, (1, I)) * fi).astype(np.float32),
        "vals": (n((E, T)) / ti).astype(np.float32),
        "offs": striped(idx),
    }


def reference(query, keys_words, keys_scales, th, dquery, os, vals, offs):
    idx = unstriped(offs)
    keysu = unpack_weight(keys_words, keys_scales, "e4m3")
    queryq = mxq(f64(query), 0, "e4m3")
    keysidxg = keysu[:, idx]
    a = queryq.T @ keysidxg
    dqueryq = mxq(f64(dquery), 0, "e4m3")
    ta = dqueryq.T @ keysidxg
    e1s = sigmoid((f64(th) - np.mean(np.square(a), axis=1, keepdims=True)) * 4.0)
    p = np.exp(a - np.max(a, axis=1, keepdims=True))
    z = np.sum(p, axis=1, keepdims=True)
    te1s = np.mean(ta * a * 2.0, axis=1, keepdims=True) * (-1.0) * 4.0 * e1s * (1.0 - e1s)
    tp = ta * p
    tz = np.sum(tp, axis=1, keepdims=True)
    tw = (tp - tz * p / z) / z * (1.0 - e1s) + te1s * (-1.0) * p / z + te1s / 512.0
    wo1 = tw * f64(os)
    wt1 = wo1.T
    vt1 = f64(vals)[:, idx].T
    wt1q = mxq(wt1, 0, "e4m3")
    vt1q = mxq(vt1, 0, "e4m3")
    o = wt1q.T @ vt1q
    return o

@@ -1,0 +1,194 @@
+from contextlib import ExitStack
+
+import concourse.mybir as mybir
+from concourse.masks import make_identity
+
+D, E, T, I, Q = 512, 512, 2048, 512, 128
+FLOPS = 2 * (2 * D * Q * I) + 2 * I * Q * E
+
+F32 = mybir.dt.float32
+BF16 = mybir.dt.bfloat16
+I32 = mybir.dt.int32
+U32 = mybir.dt.uint32
+U16 = mybir.dt.uint16
+U8 = mybir.dt.uint8
+FP8X4 = mybir.dt.float8_e4m3fn_x4
+ALU = mybir.AluOpType
+ACT = mybir.ActivationFunctionType
+
+P = 128
+PACK = 4
+BLOCKS = E // P
+
+
+def tile_attend_ttevenbyspread_kernel(tc, query, keys_words, keys_scales, th, dquery, slot_factor, vals, offs, out):
+    nc = tc.nc
+    with ExitStack() as ctx:
+        sb = ctx.enter_context(tc.tile_pool(name="sb", bufs=1))
+        ps = ctx.enter_context(tc.psum_pool(name="ps", bufs=1))
+        turn_ps = ctx.enter_context(tc.psum_pool(name="turn_ps", bufs=2))
+
+        offsets = sb.tile([P, I // 16], U16, name="offsets")
+        nc.sync.dma_start(offsets[:], offs)
+
+        th_col = sb.tile([P, 1], F32, name="th_col")
+        nc.scalar.dma_start(th_col[:], th)
+        factor_cols = sb.tile([P, PACK], F32, name="factor_cols")
+        nc.scalar.dma_start(factor_cols[:], slot_factor[0].rearrange("(p c) -> p c", c=PACK))
+
+        scale_pool = sb.tile([P, T], U8, name="scale_pool", align_bytes=64)
+        nc.vector.memset(scale_pool[:].bitcast(I32), 0)
+        for quad in range(4):
+            nc.scalar.dma_start(
+                scale_pool[32 * quad : 32 * quad + 4, :].bitcast(I32),
+                keys_scales[0, 4 * quad : 4 * quad + 4, :].bitcast(I32),
+            )
+
+        word_pool = sb.tile([P, T], U32, name="word_pool", align_bytes=64)
+        nc.sync.dma_start(word_pool[:].bitcast(I32), keys_words[0].rearrange("p n t -> p (n t)").bitcast(I32))
+
+        q_raw = [sb.tile([P, PACK, Q], F32, name="q_raw%d" % s) for s in range(2)]
+        for s, source in enumerate((query, dquery)):
+            nc.sync.dma_start(q_raw[s][:], source.rearrange("(p j) q -> p j q", j=PACK))
+
+        val_pool = [sb.tile([P, T], F32, name="val_pool%d" % b) for b in range(BLOCKS)]
+        for b in range(BLOCKS):
+            nc.sync.dma_start(val_pool[b][:], vals[b * P : (b + 1) * P, :])
+
+        ident = sb.tile([P, P], F32, name="ident")
+        make_identity(nc, ident[:])
+
+        th4 = sb.tile([P, 2], F32, name="th4")
+        nc.scalar.activation(th4[:, 0:1], th_col[:], ACT.Copy, scale=-4.0)
+        nc.scalar.activation(th4[:, 1:2], th_col[:], ACT.Copy, scale=4.0)
+
+        k_scales = sb.tile([P, I], U8, name="k_scales", align_bytes=64)
+        nc.vector.tensor_copy(k_scales[:], scale_pool[:].indirect(offsets[:]))
+        k_codes = sb.tile([P, I], U32, name="k_codes", align_bytes=64)
+        nc.vector.tensor_copy(k_codes[:], word_pool[:].indirect(offsets[:]))
+
+        q_in = sb.tile([P, 2, Q, PACK], BF16, name="q_in", align_bytes=64)
+        for s in range(2):
+            nc.scalar.copy(q_in[:, s], q_raw[s][:].rearrange("p j q -> p q j"))
+        q_codes = sb.tile([P, 2 * Q], U32, name="q_codes", align_bytes=64)
+        q_scales = sb.tile([P, 2 * Q], U8, name="q_scales", align_bytes=64)
+        nc.vector.quantize_mx(q_codes[:].bitcast(FP8X4), q_scales[:], q_in[:].rearrange("p s q j -> p (s q j)"))
+
+        a_ps = ps.tile([P, I], F32, name="a_ps")
+        ta_ps = ps.tile([P, I], F32, name="ta_ps")
+        for s, bank in enumerate((a_ps, ta_ps)):
+            cols = slice(s * Q, (s + 1) * Q)
+            nc.tensor.matmul_mx(
+                out=bank[:],
+                lhsT=q_codes[:, cols].bitcast(FP8X4),
+                lhsT_scale=q_scales[:, cols],
+                rhs=k_codes[:].bitcast(FP8X4),
+                rhs_scale=k_scales[:],
+                start=True,
+                stop=True,
+            )
+
+        factor_ps = ps.tile([P, PACK, P], F32, name="factor_ps")
+        for c in range(PACK):
+            nc.tensor.transpose(factor_ps[:, c, :], factor_cols[:, c : c + 1].to_broadcast([P, P]), ident[:])
+
+        def turn_and_quantize(permuted, label):
+            words = permuted[:].bitcast(F32)
+            turned = turn_ps.tile([P, 2, P], F32, name="turned")
+            for u in range(2):
+                nc.tensor.transpose(turned[:, u, :], words[:, u * P : (u + 1) * P], ident[:])
+            woven = sb.tile([P, P, 2], F32, name="woven_" + label, align_bytes=64)
+            nc.scalar.copy(woven[:], turned[:].rearrange("p u c -> p c u"))
+            codes = sb.tile([P, P], U32, name="codes_" + label, align_bytes=64)
+            scales = sb.tile([P, P], U8, name="scales_" + label, align_bytes=64)
+            nc.vector.quantize_mx(
+                codes[:].bitcast(FP8X4), scales[:], woven[:].rearrange("p c u -> p (c u)").bitcast(BF16)
+            )
+            return codes, scales
+
+        def gather_values(b):
+            picked = sb.tile([P, I], BF16, name="picked%d" % b, align_bytes=64)
+            nc.vector.tensor_copy(
+                picked[:].rearrange("p (u g j) -> p g u j", u=2, j=16), val_pool[b][:].indirect(offsets[:])
+            )
+            return picked
+
+        neg_a = sb.tile([P, I], F32, name="neg_a")
+        neg_max = sb.tile([P, 1], F32, name="neg_max")
+        nc.vector.tensor_scalar(neg_a[:], a_ps[:], -1.0, None, ALU.mult, ALU.min, accum_out=neg_max[:])
+
+        denominators = sb.tile([P, 3], F32, name="denominators")
+        z = denominators[:, 0:1]
+        p = sb.tile([P, I], F32, name="p")
+        nc.scalar.activation(p[:], a_ps[:], ACT.Exp, bias=neg_max[:], accum_out=z)
+
+        row = sb.tile([P, 4], F32, name="row")
+        spread = row[:, 0:1]
+        inv_z = row[:, 1:2]
+        ta_a = sb.tile([P, I], F32, name="ta_a")
+        nc.vector.scalar_tensor_tensor(ta_a[:], ta_ps[:], -8.0 / I, neg_a[:], ALU.mult, ALU.mult, accum_out=spread)
+
+        a_sq = sb.tile([P, I], F32, name="a_sq")
+        sum_sq = sb.tile([P, 1], F32, name="sum_sq")
+        nc.scalar.activation(a_sq[:], neg_a[:], ACT.Square, accum_out=sum_sq[:])
+        gate_exp = sb.tile([P, 2], F32, name="gate_exp")
+        nc.scalar.activation(gate_exp[:, 0:1], sum_sq[:], ACT.Exp, bias=th4[:, 0:1], scale=4.0 / I)
+        nc.scalar.activation(gate_exp[:, 1:2], sum_sq[:], ACT.Exp, bias=th4[:, 1:2], scale=-4.0 / I)
+
+        tp = sb.tile([P, I], F32, name="tp")
+        tz = sb.tile([P, 1], F32, name="tz")
+        nc.vector.scalar_tensor_tensor(tp[:], ta_ps[:], 1.0, p[:], ALU.mult, ALU.mult, accum_out=tz[:])
+
+        picked = [gather_values(0)]
+        values = [turn_and_quantize(picked[0], "v0")]
+
+        nc.vector.tensor_scalar(denominators[:, 1:3], gate_exp[:], 1.0, None, ALU.add)
+        nc.vector.reciprocal(row[:, 1:4], denominators[:])
+        mixed = sb.tile([P, 2], F32, name="mixed")
+        nc.vector.tensor_tensor(mixed[:], row[:, 0:2], row[:, 2:4], ALU.mult)
+        e_spread = mixed[:, 0:1]
+        softmax_share = mixed[:, 1:2]
+        shift = sb.tile([P, 1], F32, name="shift")
+        nc.vector.scalar_tensor_tensor(shift[:], tz[:], inv_z, e_spread, ALU.mult, ALU.subtract)
+        even = sb.tile([P, 1], F32, name="even")
+        nc.vector.tensor_scalar(even[:], e_spread, z, 1.0 / I, ALU.mult, ALU.mult)
+
+        factor = sb.tile([P, P, PACK], F32, name="factor")
+        nc.scalar.activation(factor[:], factor_ps[:].rearrange("p c s -> p s c"), ACT.Copy, scale=softmax_share)
+
+        centred = sb.tile([P, I], F32, name="centred")
+        nc.vector.scalar_tensor_tensor(centred[:], ta_ps[:], shift[:], p[:], ALU.subtract, ALU.mult)
+        weights = sb.tile([P, I], BF16, name="weights", align_bytes=64)
+        centred_u = centred[:].rearrange("p (g u j) -> p u g j", u=2, j=16)
+        factor_u = factor[:].rearrange("p s c -> p (s c)").rearrange("p (g u j) -> p u g j", u=2, j=16)
+        weights_u = weights[:].rearrange("p (u g j) -> p u g j", u=2, j=16)
+        for u in range(2):
+            nc.vector.scalar_tensor_tensor(
+                weights_u[:, u], centred_u[:, u], even[:], factor_u[:, u], ALU.subtract, ALU.mult
+            )
+        picked.append(gather_values(1))
+        w_codes, w_scales = turn_and_quantize(weights, "w")
+        values.append(turn_and_quantize(picked[1], "v1"))
+        for b in range(2, BLOCKS):
+            picked.append(gather_values(b))
+            values.append(turn_and_quantize(picked[b], "v%d" % b))
+
+        first_ps = ps.tile([P, (BLOCKS - 1) * P], F32, name="first_ps")
+        last_ps = ps.tile([P, P], F32, name="last_ps")
+        for b in range(BLOCKS):
+            target = first_ps[:, b * P : (b + 1) * P] if b < BLOCKS - 1 else last_ps[:]
+            nc.tensor.matmul_mx(
+                out=target,
+                lhsT=w_codes[:].bitcast(FP8X4),
+                lhsT_scale=w_scales[:],
+                rhs=values[b][0][:].bitcast(FP8X4),
+                rhs_scale=values[b][1][:],
+                start=True,
+                stop=True,
+            )
+        first_sb = sb.tile([P, (BLOCKS - 1) * P], F32, name="first_sb")
+        nc.scalar.copy(first_sb[:], first_ps[:])
+        nc.sync.dma_start(out[:, : (BLOCKS - 1) * P], first_sb[:])
+        last_sb = sb.tile([P, P], F32, name="last_sb")
+        nc.vector.tensor_copy(last_sb[:], last_ps[:])
+        nc.sync.dma_start(out[:, (BLOCKS - 1) * P :], last_sb[:])

@@ -19,6 +19,7 @@ ACT = mybir.ActivationFunctionType
 P = 128
 PACK = 4
 BLOCKS = E // P
+HALF = I // 2
 
 
 def tile_attend_ttevenbyspread_kernel(tc, query, keys_words, keys_scales, th, dquery, slot_factor, vals, offs, out):
@@ -26,169 +27,210 @@ def tile_attend_ttevenbyspread_kernel(tc, query, keys_words, keys_scales, th, dq
     with ExitStack() as ctx:
         sb = ctx.enter_context(tc.tile_pool(name="sb", bufs=1))
         ps = ctx.enter_context(tc.psum_pool(name="ps", bufs=1))
-        turn_ps = ctx.enter_context(tc.psum_pool(name="turn_ps", bufs=2))
+
+        def quantize(woven, label, slot):
+            width = woven.shape[1] // PACK
+            codes = sb.tile([P, width], U32, name="codes_" + label, tag=slot, align_bytes=64)
+            scales = sb.tile([P, width], U8, name="scales_" + label, align_bytes=64)
+            nc.vector.quantize_mx(codes[:].bitcast(FP8X4), scales[:], woven)
+            return codes, scales
 
         offsets = sb.tile([P, I // 16], U16, name="offsets")
         nc.sync.dma_start(offsets[:], offs)
-
-        th_col = sb.tile([P, 1], F32, name="th_col")
-        nc.scalar.dma_start(th_col[:], th)
-        factor_cols = sb.tile([P, PACK], F32, name="factor_cols")
-        nc.scalar.dma_start(factor_cols[:], slot_factor[0].rearrange("(p c) -> p c", c=PACK))
-
-        scale_pool = sb.tile([P, T], U8, name="scale_pool", align_bytes=64)
-        nc.vector.memset(scale_pool[:].bitcast(I32), 0)
-        for quad in range(4):
-            nc.scalar.dma_start(
-                scale_pool[32 * quad : 32 * quad + 4, :].bitcast(I32),
-                keys_scales[0, 4 * quad : 4 * quad + 4, :].bitcast(I32),
-            )
-
-        word_pool = sb.tile([P, T], U32, name="word_pool", align_bytes=64)
-        nc.sync.dma_start(word_pool[:].bitcast(I32), keys_words[0].rearrange("p n t -> p (n t)").bitcast(I32))
 
         q_raw = [sb.tile([P, PACK, Q], F32, name="q_raw%d" % s) for s in range(2)]
         for s, source in enumerate((query, dquery)):
             nc.sync.dma_start(q_raw[s][:], source.rearrange("(p j) q -> p j q", j=PACK))
 
-        val_pool = [sb.tile([P, T], F32, name="val_pool%d" % b) for b in range(BLOCKS)]
-        for b in range(BLOCKS):
-            nc.sync.dma_start(val_pool[b][:], vals[b * P : (b + 1) * P, :])
+        scale_pool = sb.tile([P, T], U8, name="scale_pool", align_bytes=64)
+        nc.gpsimd.memset(scale_pool[:].bitcast(I32), 0)
+        for quad in range(4):
+            nc.sync.dma_start(
+                scale_pool[32 * quad : 32 * quad + 4, :].bitcast(I32),
+                keys_scales[0, 4 * quad : 4 * quad + 4, :].bitcast(I32),
+            )
 
         ident = sb.tile([P, P], F32, name="ident")
         make_identity(nc, ident[:])
 
+        word_pool = sb.tile([P, T], U32, name="word_pool", align_bytes=64)
+        nc.sync.dma_start(word_pool[:].bitcast(I32), keys_words[0].rearrange("p n t -> p (n t)").bitcast(I32))
+
+        th_col = sb.tile([P, 1], F32, name="th_col")
+        nc.sync.dma_start(th_col[:], th)
+        factor_cols = sb.tile([P, PACK], F32, name="factor_cols")
+        nc.gpsimd.dma_start(factor_cols[:], slot_factor[0].rearrange("(p c) -> p c", c=PACK))
+
+        q_in = [sb.tile([P, Q, PACK], BF16, name="q_in%d" % s, align_bytes=64) for s in range(2)]
+        for s in range(2):
+            nc.scalar.activation(q_in[s][:], q_raw[s][:].rearrange("p j q -> p q j"), ACT.Copy)
         th4 = sb.tile([P, 2], F32, name="th4")
-        nc.scalar.activation(th4[:, 0:1], th_col[:], ACT.Copy, scale=-4.0)
-        nc.scalar.activation(th4[:, 1:2], th_col[:], ACT.Copy, scale=4.0)
+        nc.scalar.activation(th4[:, 0:1], th_col[:], ACT.Copy, scale=4.0)
+        nc.scalar.activation(th4[:, 1:2], th_col[:], ACT.Copy, scale=-4.0)
 
         k_scales = sb.tile([P, I], U8, name="k_scales", align_bytes=64)
         nc.vector.tensor_copy(k_scales[:], scale_pool[:].indirect(offsets[:]))
-        k_codes = sb.tile([P, I], U32, name="k_codes", align_bytes=64)
-        nc.vector.tensor_copy(k_codes[:], word_pool[:].indirect(offsets[:]))
+        q_mx = quantize(q_in[0][:].rearrange("p q j -> p (q j)"), "q", "codes_q")
+        dq_mx = quantize(q_in[1][:].rearrange("p q j -> p (q j)"), "dq", "codes_dq")
+        k_codes = sb.tile([P, I], U32, name="k_codes", tag="k_codes", align_bytes=64)
+        for h in range(2):
+            nc.vector.tensor_copy(
+                k_codes[:, h * HALF : (h + 1) * HALF], word_pool[:].indirect(offsets[:, h * HALF // 16 : (h + 1) * HALF // 16])
+            )
 
-        q_in = sb.tile([P, 2, Q, PACK], BF16, name="q_in", align_bytes=64)
-        for s in range(2):
-            nc.scalar.copy(q_in[:, s], q_raw[s][:].rearrange("p j q -> p q j"))
-        q_codes = sb.tile([P, 2 * Q], U32, name="q_codes", align_bytes=64)
-        q_scales = sb.tile([P, 2 * Q], U8, name="q_scales", align_bytes=64)
-        nc.vector.quantize_mx(q_codes[:].bitcast(FP8X4), q_scales[:], q_in[:].rearrange("p s q j -> p (s q j)"))
 
-        a_ps = ps.tile([P, I], F32, name="a_ps")
-        ta_ps = ps.tile([P, I], F32, name="ta_ps")
-        for s, bank in enumerate((a_ps, ta_ps)):
-            cols = slice(s * Q, (s + 1) * Q)
+        val_pool = [sb.tile([P, T], F32, name="val_pool%d" % b, tag="slot%d" % b, align_bytes=64) for b in range(BLOCKS)]
+        for b in range(BLOCKS):
+            nc.sync.dma_start(val_pool[b][:], vals[b * P : (b + 1) * P, :])
+
+        def score(target, rows, slots):
             nc.tensor.matmul_mx(
-                out=bank[:],
-                lhsT=q_codes[:, cols].bitcast(FP8X4),
-                lhsT_scale=q_scales[:, cols],
-                rhs=k_codes[:].bitcast(FP8X4),
-                rhs_scale=k_scales[:],
+                out=target,
+                lhsT=rows[0][:].bitcast(FP8X4),
+                lhsT_scale=rows[1][:],
+                rhs=k_codes[:, slots].bitcast(FP8X4),
+                rhs_scale=k_scales[:, slots],
                 start=True,
                 stop=True,
             )
 
-        factor_ps = ps.tile([P, PACK, P], F32, name="factor_ps")
-        for c in range(PACK):
-            nc.tensor.transpose(factor_ps[:, c, :], factor_cols[:, c : c + 1].to_broadcast([P, P]), ident[:])
+        a_ps = [ps.tile([P, HALF], F32, name="a_ps%d" % h, tag="a_ps%d" % h) for h in range(2)]
+        for h in range(2):
+            score(a_ps[h][:], q_mx, slice(h * HALF, (h + 1) * HALF))
+        ta_ps = ps.tile([P, I], F32, name="ta_ps")
+        score(ta_ps[:], dq_mx, slice(0, I))
+        ta_dealt = ta_ps[:].rearrange("q (s t) -> q t s", t=PACK)
 
-        def turn_and_quantize(permuted, label):
-            words = permuted[:].bitcast(F32)
-            turned = turn_ps.tile([P, 2, P], F32, name="turned")
-            for u in range(2):
-                nc.tensor.transpose(turned[:, u, :], words[:, u * P : (u + 1) * P], ident[:])
-            woven = sb.tile([P, P, 2], F32, name="woven_" + label, align_bytes=64)
-            nc.scalar.copy(woven[:], turned[:].rearrange("p u c -> p c u"))
-            codes = sb.tile([P, P], U32, name="codes_" + label, align_bytes=64)
-            scales = sb.tile([P, P], U8, name="scales_" + label, align_bytes=64)
-            nc.vector.quantize_mx(
-                codes[:].bitcast(FP8X4), scales[:], woven[:].rearrange("p c u -> p (c u)").bitcast(BF16)
-            )
-            return codes, scales
+        def turn(picked, label, bank, slot):
+            count = len(picked)
+            turned = ps.tile([P, count, 2, P], F32, name="turned_" + label, tag=bank)
+            for n in range(count):
+                words = picked[n][:].bitcast(F32)
+                for u in range(2):
+                    nc.tensor.transpose(turned[:, n, u, :], words[:, u : 2 * P : 2], ident[:])
+            woven = sb.tile([P, count, P, 2], F32, name="woven_" + label, tag=slot, align_bytes=64)
+            nc.scalar.copy(woven[:], turned[:].rearrange("p n u c -> p n c u"))
+            return woven[:].rearrange("p n c u -> p (n c u)").bitcast(BF16)
 
-        def gather_values(b):
-            picked = sb.tile([P, I], BF16, name="picked%d" % b, align_bytes=64)
-            nc.vector.tensor_copy(
-                picked[:].rearrange("p (u g j) -> p g u j", u=2, j=16), val_pool[b][:].indirect(offsets[:])
-            )
+        def gather_values(b, slot):
+            picked = sb.tile([P, I], BF16, name="picked%d" % b, tag=slot, align_bytes=64)
+            nc.vector.tensor_copy(picked[:], val_pool[b][:].indirect(offsets[:]))
             return picked
 
-        neg_a = sb.tile([P, I], F32, name="neg_a")
-        neg_max = sb.tile([P, 1], F32, name="neg_max")
-        nc.vector.tensor_scalar(neg_a[:], a_ps[:], -1.0, None, ALU.mult, ALU.min, accum_out=neg_max[:])
-
-        denominators = sb.tile([P, 3], F32, name="denominators")
-        z = denominators[:, 0:1]
-        p = sb.tile([P, I], F32, name="p")
-        nc.scalar.activation(p[:], a_ps[:], ACT.Exp, bias=neg_max[:], accum_out=z)
-
-        row = sb.tile([P, 4], F32, name="row")
-        spread = row[:, 0:1]
-        inv_z = row[:, 1:2]
-        ta_a = sb.tile([P, I], F32, name="ta_a")
-        nc.vector.scalar_tensor_tensor(ta_a[:], ta_ps[:], -8.0 / I, neg_a[:], ALU.mult, ALU.mult, accum_out=spread)
-
-        a_sq = sb.tile([P, I], F32, name="a_sq")
-        sum_sq = sb.tile([P, 1], F32, name="sum_sq")
-        nc.scalar.activation(a_sq[:], neg_a[:], ACT.Square, accum_out=sum_sq[:])
-        gate_exp = sb.tile([P, 2], F32, name="gate_exp")
-        nc.scalar.activation(gate_exp[:, 0:1], sum_sq[:], ACT.Exp, bias=th4[:, 0:1], scale=4.0 / I)
-        nc.scalar.activation(gate_exp[:, 1:2], sum_sq[:], ACT.Exp, bias=th4[:, 1:2], scale=-4.0 / I)
-
-        tp = sb.tile([P, I], F32, name="tp")
-        tz = sb.tile([P, 1], F32, name="tz")
-        nc.vector.scalar_tensor_tensor(tp[:], ta_ps[:], 1.0, p[:], ALU.mult, ALU.mult, accum_out=tz[:])
-
-        picked = [gather_values(0)]
-        values = [turn_and_quantize(picked[0], "v0")]
-
-        nc.vector.tensor_scalar(denominators[:, 1:3], gate_exp[:], 1.0, None, ALU.add)
-        nc.vector.reciprocal(row[:, 1:4], denominators[:])
-        mixed = sb.tile([P, 2], F32, name="mixed")
-        nc.vector.tensor_tensor(mixed[:], row[:, 0:2], row[:, 2:4], ALU.mult)
-        e_spread = mixed[:, 0:1]
-        softmax_share = mixed[:, 1:2]
-        shift = sb.tile([P, 1], F32, name="shift")
-        nc.vector.scalar_tensor_tensor(shift[:], tz[:], inv_z, e_spread, ALU.mult, ALU.subtract)
-        even = sb.tile([P, 1], F32, name="even")
-        nc.vector.tensor_scalar(even[:], e_spread, z, 1.0 / I, ALU.mult, ALU.mult)
-
-        factor = sb.tile([P, P, PACK], F32, name="factor")
-        nc.scalar.activation(factor[:], factor_ps[:].rearrange("p c s -> p s c"), ACT.Copy, scale=softmax_share)
-
-        centred = sb.tile([P, I], F32, name="centred")
-        nc.vector.scalar_tensor_tensor(centred[:], ta_ps[:], shift[:], p[:], ALU.subtract, ALU.mult)
-        weights = sb.tile([P, I], BF16, name="weights", align_bytes=64)
-        centred_u = centred[:].rearrange("p (g u j) -> p u g j", u=2, j=16)
-        factor_u = factor[:].rearrange("p s c -> p (s c)").rearrange("p (g u j) -> p u g j", u=2, j=16)
-        weights_u = weights[:].rearrange("p (u g j) -> p u g j", u=2, j=16)
-        for u in range(2):
-            nc.vector.scalar_tensor_tensor(
-                weights_u[:, u], centred_u[:, u], even[:], factor_u[:, u], ALU.subtract, ALU.mult
+        neg_a = sb.tile([P, PACK, P], F32, name="neg_a")
+        neg_max = sb.tile([P, 2], F32, name="neg_max")
+        a_sq = sb.tile([P, PACK, P], F32, name="a_sq")
+        sum_sq = sb.tile([P, 2], F32, name="sum_sq")
+        for h in range(2):
+            part = slice(h * P // 2, (h + 1) * P // 2)
+            nc.vector.tensor_scalar(
+                neg_a[:, :, part],
+                a_ps[h][:].rearrange("q (s t) -> q t s", t=PACK),
+                -1.0,
+                neg_max[:, 0:1] if h else None,
+                ALU.mult,
+                ALU.min,
+                accum_out=neg_max[:, h : h + 1],
             )
-        picked.append(gather_values(1))
-        w_codes, w_scales = turn_and_quantize(weights, "w")
-        values.append(turn_and_quantize(picked[1], "v1"))
-        for b in range(2, BLOCKS):
-            picked.append(gather_values(b))
-            values.append(turn_and_quantize(picked[b], "v%d" % b))
+            nc.scalar.activation(a_sq[:, :, part], neg_a[:, :, part], ACT.Square, accum_out=sum_sq[:, h : h + 1])
 
-        first_ps = ps.tile([P, (BLOCKS - 1) * P], F32, name="first_ps")
-        last_ps = ps.tile([P, P], F32, name="last_ps")
-        for b in range(BLOCKS):
-            target = first_ps[:, b * P : (b + 1) * P] if b < BLOCKS - 1 else last_ps[:]
+        z = sb.tile([P, 1], F32, name="z")
+        p = sb.tile([P, PACK, P], F32, name="p")
+        nc.scalar.activation(p[:], neg_a[:], ACT.Exp, scale=-1.0, bias=neg_max[:, 1:2], accum_out=z[:])
+
+        picked0 = gather_values(0, "k_codes")
+
+        gate_half = sb.tile([P, 2], F32, name="gate_half")
+        gate_exp = sb.tile([P, 2], F32, name="gate_exp")
+        for c, sign in enumerate((-1.0, 1.0)):
+            nc.scalar.activation(
+                gate_half[:, c : c + 1], sum_sq[:, 0:1], ACT.Identity, bias=th4[:, c : c + 1], scale=sign * 4.0 / I
+            )
+        for c, sign in enumerate((-1.0, 1.0)):
+            nc.scalar.activation(
+                gate_exp[:, c : c + 1], sum_sq[:, 1:2], ACT.Exp, bias=gate_half[:, c : c + 1], scale=sign * 4.0 / I
+            )
+        share_den = sb.tile([P, 1], F32, name="share_den")
+        nc.scalar.activation(share_den[:], gate_exp[:, 0:1], ACT.Identity, scale=z[:], bias=z[:])
+        denominators = sb.tile([P, 2], F32, name="denominators", tag="denominators", align_bytes=64)
+        nc.scalar.activation(denominators[:, 0:1], z[:], ACT.Copy, scale=-1.0)
+        two_plus = sb.tile([P, 1], F32, name="two_plus", tag="two_plus", align_bytes=64)
+        nc.scalar.activation(two_plus[:], gate_exp[:, 0:1], ACT.Identity, bias=2.0)
+        nc.scalar.activation(denominators[:, 1:2], gate_exp[:, 1:2], ACT.Identity, bias=two_plus[:])
+
+        share = sb.tile([P, 1], F32, name="share", tag="slot0", align_bytes=64)
+        nc.vector.reciprocal(share[:], share_den[:])
+        inverses = sb.tile([P, 2], F32, name="inverses", tag="inverses", align_bytes=64)
+        nc.vector.reciprocal(inverses[:], denominators[:])
+        neg_inv_z = inverses[:, 0:1]
+        gate_slope = inverses[:, 1:2]
+
+        tp = sb.tile([P, PACK, P], F32, name="tp")
+        tz = sb.tile([P, 1], F32, name="tz")
+        nc.vector.scalar_tensor_tensor(
+            tp[:], ta_dealt, share[:], p[:], ALU.mult, ALU.mult, accum_out=tz[:]
+        )
+
+        spread = sb.tile([P, 1], F32, name="spread")
+        ta_a = sb.tile([P, PACK, P], F32, name="ta_a", tag="denominators", align_bytes=64)
+        nc.vector.scalar_tensor_tensor(ta_a[:], ta_dealt, 8.0 / I, neg_a[:], ALU.mult, ALU.mult, accum_out=spread[:])
+
+        even_slope = sb.tile([P, 1], F32, name="even_slope")
+        nc.scalar.activation(even_slope[:], gate_slope, ACT.Copy, scale=1.0 / I)
+        tz_te = sb.tile([P, 1], F32, name="tz_te")
+        nc.scalar.activation(tz_te[:], spread[:], ACT.Identity, scale=gate_slope, bias=tz[:])
+        even = sb.tile([P, 1], F32, name="even")
+        nc.scalar.activation(even[:], spread[:], ACT.Copy, scale=even_slope[:])
+        p_factor = sb.tile([P, 1], F32, name="p_factor")
+        nc.scalar.activation(p_factor[:], tz_te[:], ACT.Copy, scale=neg_inv_z)
+        rest = sb.tile([P, PACK, P], F32, name="rest", tag="rest", align_bytes=64)
+        for half in range(2):
+            places = slice(2 * half, 2 * half + 2)
+            nc.scalar.activation(rest[:, places], p[:, places], ACT.Identity, scale=p_factor[:], bias=even[:])
+        tw_ps = ps.tile([P, PACK, Q], F32, name="tw_ps", tag="tw_ps")
+        for t in range(PACK):
+            nc.tensor.matmul(tw_ps[:, t, :], tp[:, t, :], ident[:], start=(t == 0), stop=False, is_transpose=True)
+        for t in range(PACK):
+            nc.tensor.matmul(tw_ps[:, t, :], rest[:, t, :], ident[:], start=False, stop=(t == PACK - 1), is_transpose=True)
+
+        woven0 = turn([picked0], "v0", "turned_v0", "two_plus")
+        values0 = quantize(woven0, "v0", "codes_v0")
+        picked1 = gather_values(1, "slot0")
+        picked2 = gather_values(2, "inverses")
+
+        weights = sb.tile([P, Q, PACK], BF16, name="weights", tag="slot2", align_bytes=64)
+        nc.vector.tensor_tensor(
+            weights[:],
+            tw_ps[:].rearrange("s t q -> s q t"),
+            factor_cols[:].unsqueeze(1).to_broadcast([P, Q, PACK]),
+            ALU.mult,
+        )
+        picked3 = gather_values(3, "rest")
+        woven12 = turn([picked1, picked2], "v12", "tw_ps", "woven_v12")
+        woven3 = turn([picked3], "v3", "turned_v3", "woven_v3")
+        w_codes, w_scales = quantize(weights[:].rearrange("s q t -> s (q t)"), "w", "slot3")
+        values12 = quantize(woven12, "v12", "slot2")
+        values3 = quantize(woven3, "v3", "codes_v3")
+
+        def multiply(values, target):
             nc.tensor.matmul_mx(
                 out=target,
                 lhsT=w_codes[:].bitcast(FP8X4),
                 lhsT_scale=w_scales[:],
-                rhs=values[b][0][:].bitcast(FP8X4),
-                rhs_scale=values[b][1][:],
+                rhs=values[0][:].bitcast(FP8X4),
+                rhs_scale=values[1][:],
                 start=True,
                 stop=True,
             )
-        first_sb = sb.tile([P, (BLOCKS - 1) * P], F32, name="first_sb")
-        nc.scalar.copy(first_sb[:], first_ps[:])
-        nc.sync.dma_start(out[:, : (BLOCKS - 1) * P], first_sb[:])
-        last_sb = sb.tile([P, P], F32, name="last_sb")
-        nc.vector.tensor_copy(last_sb[:], last_ps[:])
-        nc.sync.dma_start(out[:, (BLOCKS - 1) * P :], last_sb[:])
+
+        def finish(values, first_column, label, bank, copy, queue):
+            width = values[0].shape[1]
+            result_ps = ps.tile([P, width], F32, name="result_ps" + label, tag=bank)
+            multiply(values, result_ps[:])
+            result = sb.tile([P, width], F32, name="result" + label)
+            copy(result[:], result_ps[:])
+            queue.dma_start(out[:, first_column : first_column + width], result[:])
+
+        finish(values0, 0, "0", "a_ps0", nc.vector.tensor_copy, nc.sync)
+        finish(values12, P, "12", "a_ps1", nc.scalar.copy, nc.scalar)
+        finish(values3, 3 * P, "3", "turned_v0", nc.vector.tensor_copy, nc.sync)

from contextlib import ExitStack

import concourse.mybir as mybir
from concourse.masks import make_identity

D, E, T, I, Q = 512, 512, 2048, 512, 128
FLOPS = 2 * (2 * D * Q * I) + 2 * I * Q * E

F32 = mybir.dt.float32
BF16 = mybir.dt.bfloat16
I32 = mybir.dt.int32
U32 = mybir.dt.uint32
U16 = mybir.dt.uint16
U8 = mybir.dt.uint8
FP8X4 = mybir.dt.float8_e4m3fn_x4
ALU = mybir.AluOpType
ACT = mybir.ActivationFunctionType

P = 128
PACK = 4
BLOCKS = E // P
HALF = I // 2


def tile_attend_ttevenbyspread_kernel(tc, query, keys_words, keys_scales, th, dquery, slot_factor, vals, offs, out):
    nc = tc.nc
    with ExitStack() as ctx:
        sb = ctx.enter_context(tc.tile_pool(name="sb", bufs=1))
        ps = ctx.enter_context(tc.psum_pool(name="ps", bufs=1))

        def quantize(woven, label, slot):
            width = woven.shape[1] // PACK
            codes = sb.tile([P, width], U32, name="codes_" + label, tag=slot, align_bytes=64)
            scales = sb.tile([P, width], U8, name="scales_" + label, align_bytes=64)
            nc.vector.quantize_mx(codes[:].bitcast(FP8X4), scales[:], woven)
            return codes, scales

        offsets = sb.tile([P, I // 16], U16, name="offsets")
        nc.sync.dma_start(offsets[:], offs)

        q_raw = [sb.tile([P, PACK, Q], F32, name="q_raw%d" % s) for s in range(2)]
        for s, source in enumerate((query, dquery)):
            nc.sync.dma_start(q_raw[s][:], source.rearrange("(p j) q -> p j q", j=PACK))

        scale_pool = sb.tile([P, T], U8, name="scale_pool", align_bytes=64)
        nc.gpsimd.memset(scale_pool[:].bitcast(I32), 0)
        for quad in range(4):
            nc.sync.dma_start(
                scale_pool[32 * quad : 32 * quad + 4, :].bitcast(I32),
                keys_scales[0, 4 * quad : 4 * quad + 4, :].bitcast(I32),
            )

        ident = sb.tile([P, P], F32, name="ident")
        make_identity(nc, ident[:])

        word_pool = sb.tile([P, T], U32, name="word_pool", align_bytes=64)
        nc.sync.dma_start(word_pool[:].bitcast(I32), keys_words[0].rearrange("p n t -> p (n t)").bitcast(I32))

        th_col = sb.tile([P, 1], F32, name="th_col")
        nc.sync.dma_start(th_col[:], th)
        factor_cols = sb.tile([P, PACK], F32, name="factor_cols")
        nc.gpsimd.dma_start(factor_cols[:], slot_factor[0].rearrange("(p c) -> p c", c=PACK))

        q_in = [sb.tile([P, Q, PACK], BF16, name="q_in%d" % s, align_bytes=64) for s in range(2)]
        for s in range(2):
            nc.scalar.activation(q_in[s][:], q_raw[s][:].rearrange("p j q -> p q j"), ACT.Copy)
        th4 = sb.tile([P, 2], F32, name="th4")
        nc.scalar.activation(th4[:, 0:1], th_col[:], ACT.Copy, scale=4.0)
        nc.scalar.activation(th4[:, 1:2], th_col[:], ACT.Copy, scale=-4.0)

        k_scales = sb.tile([P, I], U8, name="k_scales", align_bytes=64)
        nc.vector.tensor_copy(k_scales[:], scale_pool[:].indirect(offsets[:]))
        q_mx = quantize(q_in[0][:].rearrange("p q j -> p (q j)"), "q", "codes_q")
        dq_mx = quantize(q_in[1][:].rearrange("p q j -> p (q j)"), "dq", "codes_dq")
        k_codes = sb.tile([P, I], U32, name="k_codes", tag="k_codes", align_bytes=64)
        for h in range(2):
            nc.vector.tensor_copy(
                k_codes[:, h * HALF : (h + 1) * HALF], word_pool[:].indirect(offsets[:, h * HALF // 16 : (h + 1) * HALF // 16])
            )


        val_pool = [sb.tile([P, T], F32, name="val_pool%d" % b, tag="slot%d" % b, align_bytes=64) for b in range(BLOCKS)]
        for b in range(BLOCKS):
            nc.sync.dma_start(val_pool[b][:], vals[b * P : (b + 1) * P, :])

        def score(target, rows, slots):
            nc.tensor.matmul_mx(
                out=target,
                lhsT=rows[0][:].bitcast(FP8X4),
                lhsT_scale=rows[1][:],
                rhs=k_codes[:, slots].bitcast(FP8X4),
                rhs_scale=k_scales[:, slots],
                start=True,
                stop=True,
            )

        a_ps = [ps.tile([P, HALF], F32, name="a_ps%d" % h, tag="a_ps%d" % h) for h in range(2)]
        for h in range(2):
            score(a_ps[h][:], q_mx, slice(h * HALF, (h + 1) * HALF))
        ta_ps = ps.tile([P, I], F32, name="ta_ps")
        score(ta_ps[:], dq_mx, slice(0, I))
        ta_dealt = ta_ps[:].rearrange("q (s t) -> q t s", t=PACK)

        def turn(picked, label, bank, slot):
            count = len(picked)
            turned = ps.tile([P, count, 2, P], F32, name="turned_" + label, tag=bank)
            for n in range(count):
                words = picked[n][:].bitcast(F32)
                for u in range(2):
                    nc.tensor.transpose(turned[:, n, u, :], words[:, u : 2 * P : 2], ident[:])
            woven = sb.tile([P, count, P, 2], F32, name="woven_" + label, tag=slot, align_bytes=64)
            nc.scalar.copy(woven[:], turned[:].rearrange("p n u c -> p n c u"))
            return woven[:].rearrange("p n c u -> p (n c u)").bitcast(BF16)

        def gather_values(b, slot):
            picked = sb.tile([P, I], BF16, name="picked%d" % b, tag=slot, align_bytes=64)
            nc.vector.tensor_copy(picked[:], val_pool[b][:].indirect(offsets[:]))
            return picked

        neg_a = sb.tile([P, PACK, P], F32, name="neg_a")
        neg_max = sb.tile([P, 2], F32, name="neg_max")
        a_sq = sb.tile([P, PACK, P], F32, name="a_sq")
        sum_sq = sb.tile([P, 2], F32, name="sum_sq")
        for h in range(2):
            part = slice(h * P // 2, (h + 1) * P // 2)
            nc.vector.tensor_scalar(
                neg_a[:, :, part],
                a_ps[h][:].rearrange("q (s t) -> q t s", t=PACK),
                -1.0,
                neg_max[:, 0:1] if h else None,
                ALU.mult,
                ALU.min,
                accum_out=neg_max[:, h : h + 1],
            )
            nc.scalar.activation(a_sq[:, :, part], neg_a[:, :, part], ACT.Square, accum_out=sum_sq[:, h : h + 1])

        z = sb.tile([P, 1], F32, name="z")
        p = sb.tile([P, PACK, P], F32, name="p")
        nc.scalar.activation(p[:], neg_a[:], ACT.Exp, scale=-1.0, bias=neg_max[:, 1:2], accum_out=z[:])

        picked0 = gather_values(0, "k_codes")

        gate_half = sb.tile([P, 2], F32, name="gate_half")
        gate_exp = sb.tile([P, 2], F32, name="gate_exp")
        for c, sign in enumerate((-1.0, 1.0)):
            nc.scalar.activation(
                gate_half[:, c : c + 1], sum_sq[:, 0:1], ACT.Identity, bias=th4[:, c : c + 1], scale=sign * 4.0 / I
            )
        for c, sign in enumerate((-1.0, 1.0)):
            nc.scalar.activation(
                gate_exp[:, c : c + 1], sum_sq[:, 1:2], ACT.Exp, bias=gate_half[:, c : c + 1], scale=sign * 4.0 / I
            )
        share_den = sb.tile([P, 1], F32, name="share_den")
        nc.scalar.activation(share_den[:], gate_exp[:, 0:1], ACT.Identity, scale=z[:], bias=z[:])
        denominators = sb.tile([P, 2], F32, name="denominators", tag="denominators", align_bytes=64)
        nc.scalar.activation(denominators[:, 0:1], z[:], ACT.Copy, scale=-1.0)
        two_plus = sb.tile([P, 1], F32, name="two_plus", tag="two_plus", align_bytes=64)
        nc.scalar.activation(two_plus[:], gate_exp[:, 0:1], ACT.Identity, bias=2.0)
        nc.scalar.activation(denominators[:, 1:2], gate_exp[:, 1:2], ACT.Identity, bias=two_plus[:])

        share = sb.tile([P, 1], F32, name="share", tag="slot0", align_bytes=64)
        nc.vector.reciprocal(share[:], share_den[:])
        inverses = sb.tile([P, 2], F32, name="inverses", tag="inverses", align_bytes=64)
        nc.vector.reciprocal(inverses[:], denominators[:])
        neg_inv_z = inverses[:, 0:1]
        gate_slope = inverses[:, 1:2]

        tp = sb.tile([P, PACK, P], F32, name="tp")
        tz = sb.tile([P, 1], F32, name="tz")
        nc.vector.scalar_tensor_tensor(
            tp[:], ta_dealt, share[:], p[:], ALU.mult, ALU.mult, accum_out=tz[:]
        )

        spread = sb.tile([P, 1], F32, name="spread")
        ta_a = sb.tile([P, PACK, P], F32, name="ta_a", tag="denominators", align_bytes=64)
        nc.vector.scalar_tensor_tensor(ta_a[:], ta_dealt, 8.0 / I, neg_a[:], ALU.mult, ALU.mult, accum_out=spread[:])

        even_slope = sb.tile([P, 1], F32, name="even_slope")
        nc.scalar.activation(even_slope[:], gate_slope, ACT.Copy, scale=1.0 / I)
        tz_te = sb.tile([P, 1], F32, name="tz_te")
        nc.scalar.activation(tz_te[:], spread[:], ACT.Identity, scale=gate_slope, bias=tz[:])
        even = sb.tile([P, 1], F32, name="even")
        nc.scalar.activation(even[:], spread[:], ACT.Copy, scale=even_slope[:])
        p_factor = sb.tile([P, 1], F32, name="p_factor")
        nc.scalar.activation(p_factor[:], tz_te[:], ACT.Copy, scale=neg_inv_z)
        rest = sb.tile([P, PACK, P], F32, name="rest", tag="rest", align_bytes=64)
        for half in range(2):
            places = slice(2 * half, 2 * half + 2)
            nc.scalar.activation(rest[:, places], p[:, places], ACT.Identity, scale=p_factor[:], bias=even[:])
        tw_ps = ps.tile([P, PACK, Q], F32, name="tw_ps", tag="tw_ps")
        for t in range(PACK):
            nc.tensor.matmul(tw_ps[:, t, :], tp[:, t, :], ident[:], start=(t == 0), stop=False, is_transpose=True)
        for t in range(PACK):
            nc.tensor.matmul(tw_ps[:, t, :], rest[:, t, :], ident[:], start=False, stop=(t == PACK - 1), is_transpose=True)

        woven0 = turn([picked0], "v0", "turned_v0", "two_plus")
        values0 = quantize(woven0, "v0", "codes_v0")
        picked1 = gather_values(1, "slot0")
        picked2 = gather_values(2, "inverses")

        weights = sb.tile([P, Q, PACK], BF16, name="weights", tag="slot2", align_bytes=64)
        nc.vector.tensor_tensor(
            weights[:],
            tw_ps[:].rearrange("s t q -> s q t"),
            factor_cols[:].unsqueeze(1).to_broadcast([P, Q, PACK]),
            ALU.mult,
        )
        picked3 = gather_values(3, "rest")
        woven12 = turn([picked1, picked2], "v12", "tw_ps", "woven_v12")
        woven3 = turn([picked3], "v3", "turned_v3", "woven_v3")
        w_codes, w_scales = quantize(weights[:].rearrange("s q t -> s (q t)"), "w", "slot3")
        values12 = quantize(woven12, "v12", "slot2")
        values3 = quantize(woven3, "v3", "codes_v3")

        def multiply(values, target):
            nc.tensor.matmul_mx(
                out=target,
                lhsT=w_codes[:].bitcast(FP8X4),
                lhsT_scale=w_scales[:],
                rhs=values[0][:].bitcast(FP8X4),
                rhs_scale=values[1][:],
                start=True,
                stop=True,
            )

        def finish(values, first_column, label, bank, copy, queue):
            width = values[0].shape[1]
            result_ps = ps.tile([P, width], F32, name="result_ps" + label, tag=bank)
            multiply(values, result_ps[:])
            result = sb.tile([P, width], F32, name="result" + label)
            copy(result[:], result_ps[:])
            queue.dma_start(out[:, first_column : first_column + width], result[:])

        finish(values0, 0, "0", "a_ps0", nc.vector.tensor_copy, nc.sync)
        finish(values12, P, "12", "a_ps1", nc.scalar.copy, nc.scalar)
        finish(values3, 3 * P, "3", "turned_v0", nc.vector.tensor_copy, nc.sync)
